import numpy as np, ml_dtypes
CORES = [9,25,41,57]
N = 4
BF = ml_dtypes.bfloat16
M, L, CAP, VI, ST = 3584, 256, 192, 3, 4
W = M + (VI - 1) * L
def weights(rng):
    w = rng.integers(0, 64, (N, 8, 16)); o = np.argsort(rng.random((N, 8, 16)), axis=-1)
    a = o[..., :1] == np.arange(16); b = o[..., 1:2] == np.arange(16)
    return np.where(a, 1, np.where(b, 16, w)), a[:, :, None], b[:, :, None]
def aim(v, w, a, b, t):
    v = np.where(a | b, 0, v); need = (t - np.sum(v * w[:, :, None], axis=-1)) & 63
    return v + a * (need & 15)[..., None] + b * (need >> 4)[..., None]
def shake(rng, v, k, top):
    return np.clip(v + np.floor((2 * k + 1) * rng.random(v.shape)).astype(np.int64) - k, 0, top)
def homes(rng, e):
    t = (64 * rng.random((N, 8, M)) ** e).astype(np.int64)
    t = (t * (2 * rng.integers(0, 32, (N, 8, 1)) + 1) + rng.integers(0, 64, (N, 8, 1))) & 63
    t[:, :, 1:65] = np.arange(64); return t
def points(rng, w, a, b, top):
    tree = homes(rng, rng.choice(np.array([1.0, 1.5, 2.0, 3.0]), (N, 8, 1)))
    mid = rng.integers(0, top + 1, (N, 8, 64, 16)); k = rng.integers(0, 9, (N, 8, M, 1)); k[:, :, 1:65] = 0
    v = shake(rng, np.take_along_axis(mid, tree[..., None], 2), k, top)
    far = rng.random((N, 8, M, 1)) < 0.3; far[:, :, 1:65] = False
    return tree, aim(np.where(far, rng.integers(0, top + 1, v.shape), v), w, a, b, tree)
def grow(v, tree):
    x = v.astype(np.int32); c = np.zeros(N * 8 * M * 16, np.int64)
    R, g, n = np.nonzero(np.broadcast_to(np.arange(M) > 64, (N, 8, M))); at = tree[R, g, n] + 1
    for _ in range(24):
        if len(n) == 0: break
        band = np.add.reduce(np.abs(x[R, g, n] - x[R, g, at]), axis=-1) >> 4
        key = ((R * 8 + g) * M + at) * 16 + band
        u, i = np.unique(key, return_index=True); c[u] = n[i]
        more = np.ones(len(n), bool); more[i] = False
        R, g, n, at = R[more], g[more], n[more], c[key[more]]
    return c.reshape(N, 8, M, 16)
def queries(rng, v, tree, w, a, b):
    o = rng.integers(1, M, (N, 8, VI * L)); k = rng.integers(0, 7, (N, 8, VI * L, 1))
    s = shake(rng, np.take_along_axis(v, o[..., None], 2), k, 15)
    s = np.where(rng.random((N, 8, VI * L, 1)) < 0.25, rng.integers(0, 16, s.shape), s)
    return aim(s, w, a, b, np.take_along_axis(tree, o, 2))
def radii(rng):
    z = (N, 8, VI * L)
    return np.where(rng.random(z) < 0.7, rng.integers(100, 256, z), rng.integers(0, 100, z))
def full(v):
    return np.ascontiguousarray(v.transpose(0, 1, 3, 2)).reshape(N, 128, -1)
def pack(v, c, s, w, r0, th):
    return {"pt": full(v).astype(np.float32).astype(BF), "ch": full(c).astype(np.int32), "q": full(s).astype(np.float32).astype(BF),
            "w": np.ascontiguousarray(w.reshape(N, 128, 1)).astype(np.int32), "r0": r0.astype(np.int32), "th": np.repeat(th, 16, axis=1)[..., None].astype(np.int32)}
def setup_inputs(rng):
    w, a, b = weights(rng); tree, v = points(rng, w, a, b, 15)
    return pack(v, grow(v, tree), queries(rng, v, tree, w, a, b), w, radii(rng), rng.integers(20, 60, (N, 8)))
def setup_inputs_room(rng):
    w, a, b = weights(rng); tree, v = points(rng, w, a, b, 10); z = (N, 8, VI * L)
    n = rng.choice(np.array([0, 1, CAP - 1, CAP, CAP + 1, L]), (N, 8)); n[0] = (CAP, CAP + 1, L, CAP - 1, 1, 0, CAP, CAP + 1); n[:, 2] = L
    n = np.concatenate([n[:, :, None], np.full((N, 8, VI - 1), L // 2)], axis=2)
    hot = (np.argsort(rng.random((N, 8, VI, L)), axis=-1) < n[..., None]).reshape(z)
    s = np.where(hot[..., None], rng.integers(12, 16, z + (16,)), queries(rng, v, tree, w, a, b))
    r0 = np.where(hot, rng.choice(np.array([20, 21, 255, 255, 255]), z), rng.integers(0, 20, z))
    return pack(v, grow(v, tree), s, w, r0, np.full((N, 8), 20))
def setup_inputs_knots(rng):
    w, a, b = weights(rng); v = rng.integers(0, 16, (N, 8, M, 16)); v[:, 1::2] = v[:, 1::2][:, :, rng.integers(0, 37, M)]
    dens = rng.choice(np.array([1.0, 0.6, 0.2]), (N, 8, 1, 1)); dens[:, 0] = 1.0; dens[:, 1] = 0.2; dens[:, 2] = 0.3
    c = np.where(rng.random((N, 8, M, 16)) < dens, rng.integers(1, M, (N, 8, M, 16)), 0)
    c[:, 3] = rng.choice(np.array([0, 1, 64, 65, M - 1]), (N, M, 16))
    c[:, 5] = np.where(rng.random((N, M, 16)) < 0.5, np.arange(M)[:, None], c[:, 5])
    x = rng.integers(1, M, (N, M, 2)); e = np.arange(16) - rng.integers(1, 6, (N, M, 1)); j = rng.choice(np.array([-1, 3, 4]), (N, M, 1))
    some = rng.random((N, M, 1)) < 0.4; some[:, 1:65] = True
    c[:, 6] = some * np.where((e >= 0) & (e < 3), x[:, :, :1], np.where(e == j, x[:, :, 1:], 0)); c[:, :, 0] = 0
    return pack(v, c, queries(rng, v, rng.integers(0, 64, (N, 8, M)), w, a, b), w, radii(rng), rng.integers(20, 80, (N, 8)))
def setup_inputs_ties(rng):
    w = rng.integers(0, 64, (N, 8, 16)); v = 4 * rng.integers(0, 4, (N, 8, M, 16)); tree = homes(rng, 1.0); z = (N, 8, VI * L)
    s = np.take_along_axis(v, rng.integers(1, M, z)[..., None], 2); s = np.where(rng.random(s.shape) < 0.3, 4 * rng.integers(0, 4, s.shape), s)
    s = np.where(rng.random(s.shape) < 0.01, 15, s); s[:, ::2, 1::2] = s[:, ::2, ::2]
    r0 = np.where(rng.random(z) < 0.4, 16 * rng.integers(3, 9, z) + rng.choice(np.array([-1, 1]), z), 4 * rng.integers(10, 40, z))
    return pack(v, grow(v, tree), s, w, r0, 4 * rng.integers(8, 15, (N, 8)))
def setup_inputs_ends(rng):
    w, a, b = weights(rng); tree, v = points(rng, w, a, b, 15); n = np.arange(L)
    v[:, 4, 65:65 + L] = rng.integers(0, 16, (N, L, 16)); tree[:, 4, 65:65 + L] = n & 63; v = aim(v, w, a, b, tree)
    s = queries(rng, v, tree, w, a, b); s[:, 4, :L] = v[:, 4, 65:65 + L]
    w[:, 1] = 0; w[:, 2] = 63; v[:, :, 1] = 0; v[:, :, 64] = 15; v[:, :, M - 1] = 15; v[:, 3, 1:65] = 0
    c = grow(v, tree); c[:, :, 1, 15] = M - 1; c[:, 3] = 0; c[:, 4, 65:] = 0; c[:, 4, 1 + (n & 63), 4 * (n >> 6) + 2] = 65 + n
    R = np.arange(N); z = 1 + ((15 * np.sum(w[:, 7], axis=-1)) & 63)
    v[R, 7, z] = 0; v[:, 7, 65] = 0; v[:, 7, 66] = 15
    c[R, 7, z] = 0; c[R, 7, z, 9] = 65; c[:, 7, 65] = 0; c[:, 7, 65, 4] = 66
    s[:, 1, ::3] = 15; s[:, 3, ::2] = 15; s[:, 3, 1::4] = rng.integers(14, 16, s[:, 3, 1::4].shape); s[:, 7, ::4] = 15
    s[:, :, 0] = 15; s[:, :, L - 1] = 0
    r0 = rng.choice(np.array([0, 1, 15, 16, 17, 120, 254, 255]), (N, 8, VI * L)); high = np.array([240, 241, 255])
    r0[:, 3, ::2] = rng.choice(high, r0[:, 3, ::2].shape); r0[:, 3, 1::4] = rng.choice(np.array([191, 192, 239, 240, 241, 255]), r0[:, 3, 1::4].shape)
    r0[:, 4, :L] = 255; r0[:, 7, ::4] = rng.choice(high, r0[:, 7, ::4].shape); r0[:, :, 0] = 255; r0[:, :, L - 1] = 255
    th = rng.choice(np.array([0, 1, 16, 30, 240]), (N, 8)); th[:, 0] = 0; th[:, 3] = np.array([0, 240, 241, 255])[R & 3]; th[:, 4] = 0; th[:, 5] = 255; th[:, 6] = 240
    return pack(v, c, s, w, r0, th)
def setup_inputs_spread(rng):
    w = rng.integers(0, 64, (N, 8, 16)); e = rng.choice(np.array([0.25, 0.5, 1.0, 2.0, 4.0]), (N, 8, 1, 16))
    v = (16 * rng.random((N, 8, M, 16)) ** e).astype(np.int64); s = (16 * rng.random((N, 8, VI * L, 16)) ** e).astype(np.int64)
    c = grow(v, homes(rng, 4.0)); c = np.where(rng.random(c.shape) < 0.1, rng.integers(0, M, c.shape), c); c[:, :, 0] = 0
    th = np.exp2(7 * rng.random((N, 8))).astype(np.int64); th[:, 0] = 8
    return pack(np.clip(v, 0, 15), c, np.clip(s, 0, 15), w, rng.integers(0, 256, (N, 8, VI * L)), th)
def check_inputs(d):
    bad = []
    for k in ("pt", "q"):
        x = np.asarray(d[k]).astype(np.float32)
        if not (np.all(x >= 0) and np.all(x <= 15) and np.all(x == np.floor(x))): bad.append("whole numbers from 0 to 15 in " + k)
    for k, hi in (("ch", M - 1), ("w", 63), ("r0", 255), ("th", 255)):
        if np.min(d[k]) < 0 or np.max(d[k]) > hi: bad.append("range of " + k)
    if np.any(np.asarray(d["ch"])[:, :, 0] != 0): bad.append("column 0 of ch")
    x = np.asarray(d["th"]).reshape(-1, 16)
    if np.any(x != x[:, :1]): bad.append("one threshold a group")
    return bad
def dist(u, v):
    return np.add.reduce(np.abs(u - v), axis=-1)
def inside(D, rho):
    i = np.arange(16); return (16 * i <= (D + rho)[..., None]) & (16 * i + 15 >= (D - rho)[..., None])
def at(k, i):
    return np.take_along_axis(k, i[..., None], -1)[..., 0]
def reference(pt, ch, q, w, r0, th):
    X = np.zeros((N, 8, W, 16), np.int32); X[:, :, :M] = pt.astype(np.float32).astype(np.int32).reshape(N, 8, 16, M).transpose(0, 1, 3, 2)
    C = np.zeros((N, 8, W, 16), np.int32); C[:, :, :M] = ch.reshape(N, 8, 16, M).transpose(0, 1, 3, 2)
    Q = np.ascontiguousarray(q.astype(np.float32).astype(np.int32).reshape(N, 8, 16, VI * L).transpose(0, 1, 3, 2))
    wt = w.astype(np.int32).reshape(N, 8, 1, 16); lim = th.reshape(N, 8, 16)[:, :, :1]
    a, b, ln = np.ogrid[0:N, 0:8, 0:L]; far_off = 1000
    yr, yb, yp, held = [], [], [], None
    for t in range(VI):
        v = np.array(Q[:, :, t * L:(t + 1) * L]); rho = np.array(r0[:, :, t * L:(t + 1) * L]).astype(np.int32); best = np.zeros((N, 8, L), np.int32)
        if held is not None:
            hv, hr, hb, sent, place = held; h = np.nonzero(sent); to = ((h[0] + 1) % N, h[1], place[h])
            v[to] = hv[h]; rho[to] = hr[h]; best[to] = hb[h]
        kid = np.zeros((N, 8, ST + 1, L, 16), np.int32); far = np.zeros((N, 8, ST + 1, L, 16), np.int32); own = np.zeros((N, 8, ST + 1, L), np.int32)
        lev = np.zeros((N, 8, L), np.int64); push = np.ones((N, 8, L), bool)
        m = 1 + (np.add.reduce(wt * v, axis=-1) & 63); D = dist(X[a, b, m], v)
        for s in range(ST + 1):
            if s > 0:
                k = kid[a, b, lev, ln]; f = far[a, b, lev, ln]; ok = (k > 0) & inside(own[a, b, lev, ln], rho)
                i = np.argmin(np.where(ok, f, far_off), axis=-1); push = np.any(ok, axis=-1)
                m = np.where(push, at(k, i), 0); D = np.where(push, at(f, i), far_off)
                h = np.nonzero(push); kid[h[0], h[1], lev[h], h[2], i[h]] = 0
                lev = np.where(push, lev + 1, np.maximum(lev - 1, 0))
            P = np.where(inside(D, rho) & push[..., None], C[a, b, m], 0)
            F = dist(X[a[..., None], b[..., None], P], v[:, :, :, None])
            h = np.nonzero(push); e = (h[0], h[1], lev[h], h[2])
            kid[e] = P[h]; far[e] = F[h]; own[e] = D[h]
            key = np.concatenate([D[..., None], np.where(P > 0, F, far_off)], axis=-1); node = np.concatenate([m[..., None], P], axis=-1)
            i = np.argmin(key, axis=-1); least = at(key, i); better = least < rho
            best = np.where(better, 4096 * a + at(node, i), best); rho = np.where(better, least, rho)
        yr.append(rho); yb.append(best)
        if t == VI - 1: break
        goes = rho >= lim; here = (best > 0) & (best >> 12 == a); node = np.where(here, best & 4095, 0); row = rho >> 4
        can = goes & here & (C[a, b, node, row] == 0)
        earlier = np.arange(L)[None, :] < np.arange(L)[:, None]
        win = can & ~np.any((node[:, :, :, None] == node[:, :, None, :]) & can[:, :, None, :] & earlier, axis=-1)
        X[:, :, M + t * L:M + (t + 1) * L] = v; h = np.nonzero(win); C[h[0], h[1], node[h], row[h]] = M + t * L + h[2]
        yp.append(np.where(win, node, 0))
        place = np.add.accumulate(goes.astype(np.int64), axis=2) - 1
        held = (v, rho, best, goes & (place < CAP), place)
    return {"yr": np.concatenate(yr, axis=2).astype(np.float32), "yb": np.concatenate(yb, axis=2).astype(np.float32), "yp": np.concatenate(yp, axis=2).astype(np.float32)}

from concourse.mybir import AluOpType as OP, ActivationFunctionType as AF

N, L, CAP, M, VI = 4, 256, 192, 3584, 3
B24 = float(2 ** 24)
SC = float(2 ** 26)
BIG = float(2 ** 60)
GSC = (3, 6)
NCH = 4
SCH = ((1, 3), (1, 3))
ROOM = 4096 + 256
QSC = 16

SCRATCH = {}
PS = set()
VIRT = {}
POOL = {"float32": ["poolf", 0], "int32": ["pooli", 0], "bfloat16": ["poolb", 0], "uint16": ["poolu", 0]}


def _own(name, cols, dt="float32"):
    SCRATCH[name] = ("sbuf", [128, cols], dt)
    VIRT[name] = (name, 0, cols)


def _s(name, cols, dt="float32"):
    p = POOL[dt]
    VIRT[name] = (p[0], p[1], cols)
    p[1] += (cols + 15) // 16 * 16


for _n in ("VB", "KP0", "KP1", "LI0", "LI1", "MA", "MB", "MC"):
    SCRATCH[_n] = ("psum", [128, 512], "float32")
    VIRT[_n] = (_n, 0, 512)
    PS.add(_n)
_own("PT", 4096, "bfloat16"); _own("CHI", M, "int32"); _own("CH", ROOM); _own("QF", 768, "bfloat16")
_own("wi", 8, "int32"); _own("thi", 8, "int32"); _own("r0i", 768, "int32")
_own("Q16a", 4096, "bfloat16"); _own("Q16b", 4096, "bfloat16"); _own("DIFF", 4096, "bfloat16")
for _t in "01":
    _own("SND" + _t, CAP + L, "int32"); _own("RCV" + _t, L, "int32")
for _t in "012":
    _own("or" + _t, 256); _own("ob" + _t, 256); _own("op" + _t, 256)
for _n, _c in (("r0f", 768), ("wf", 2), ("thf", 2), ("pf", 4), ("jf", 128), ("j15", 128), ("c8", 8), ("IDF", 128), ("DM", 256),
               ("LC", 8), ("RAMP", 128), ("MX", 128), ("D0", 256), ("biasc", 2), ("biasr", 2), ("TH", 16), ("KI", 16), ("K192", 16),
               ("K4096", 16), ("NID0", 256), ("NID1", 256), ("ONESF", 128), ("selj", 2048), ("SELR", 16), ("R0P1", 48),
               ("C24", 8), ("BEST0", 16), ("VF", 112), ("VZ", 112), ("LF", 112), ("RHO", 16), ("ad", 16), ("bn", 16), ("BEST", 16),
               ("pl", 16), ("go", 16), ("gd", 16), ("PN", 16), ("emp", 16), ("can", 16), ("win", 16), ("YP", 16), ("gq", 16),
               ("LBD", 256), ("Z2", 256), ("PK", 256), ("X", 256), ("GC", 256), ("M1", 256), ("OHG", 256), ("OC", 256),
               ("VAL", 256), ("LBD2", 256), ("Z3", 256), ("RV", 256), ("RT", 256), ("RF", 256), ("EF", 384)):
    _s(_n, _c)
for _n, _c in (("pi", 4), ("ji", 128), ("j15i", 128), ("V", 112), ("VI", 112), ("PI", 16), ("PJ", 16), ("hi6", 16), ("lo6", 16),
               ("RI", 256), ("RS", 256)):
    _s(_n, _c, "int32")
for _n, _c in [("IDB", 128), ("NIDB", 128), ("BLK", 8), ("BLK0", 8), ("WB", 8), ("TRI", 128), ("LTRI", 128), ("ONESB", 128),
               ("THM", 128), ("SELH", 2048), ("QV1", 256), ("QV2", 256), ("FARB", 16), ("NQ", 32), ("NQT", 128), ("RHT", 256),
               ("BC0", 128), ("CANB", 16)] + [("EQ%d" % _e, 384) for _e in range(8)]:
    _s(_n, _c, "bfloat16")
for _n in ("OFFP", "GO1", "GO2"):
    _s(_n, 16, "uint16")
for _h in "01":
    for _n, _c, _d in (("si", 8, "int32"), ("sj", 8, "int32"), ("RTL", 8, "float32"), ("SBD", 128, "float32"), ("RBD", 128, "float32"),
                       ("Z", 128, "float32"), ("OFF", 8, "uint16"), ("DR", 128, "bfloat16"), ("FB0", 8, "float32"), ("FB1", 8, "float32"),
                       ("E", 128, "float32"), ("A", 128, "float32"), ("Tf", 8, "int32"), ("u", 128, "float32"),
                       ("Pf", 128, "float32"), ("PU", 128, "uint16"), ("KU", 128, "float32"), ("KS", 128, "float32"), ("u2", 128, "float32"),
                       ("KM", 128, "float32"), ("MS", 128, "float32"), ("OH", 128, "float32"), ("FO", 128, "float32"), ("pm", 128, "float32"),
                       ("lo", 8, "int32"), ("lp", 8, "int32"), ("ri", 8, "float32"), ("rx", 8, "float32"), ("rho", 8, "float32")):
        _s(_n + _h, _c, _d)
for _d in POOL:
    SCRATCH[POOL[_d][0]] = ("sbuf", [128, POOL[_d][1]], _d)

NDMA = 26
SEMAPHORES = ["cv", "ct", "cs", "cg"] + ["d%d" % i for i in range(NDMA)] + ["arr0", "arr1", "sent0", "sent1"]


def rank_program(g, core, T, topo):
    rank = T.rank_of(core)
    if rank is None:
        return
    ops = []
    hist = {}
    ndma = [0]
    rot = [0]

    def b(name, lo=0, hi=None, st=1, rows=None):
        buf, o, c = VIRT[name]
        hi = c if hi is None else hi
        p = slice(None) if rows is None else slice(0, rows)
        return (name, lo, hi, st, T[buf][p, o + lo:o + hi:st] if st > 1 else T[buf][p, o + lo:o + hi])

    def ind(w, o):
        return (w[0], w[1], w[2], 1, w[4].indirect(o[4]))

    def clash(x, y):
        if x[1] <= y[0] or y[1] <= x[0]:
            return False
        return not (x[2] == y[2] and x[2] > 1 and (x[0] - y[0]) % x[2])

    def op(q, call, reads, writes, cost, kind="c", ext=None):
        n = len(ops)
        deps = set()
        after = set()
        both = [(False, o) for o in reads] + [(True, o) for o in writes]
        for w, o in both:
            r = (o[1], o[2], o[3])
            for (r2, w2, n2) in hist.get(o[0], ()):
                if o[0] in PS and q == "t" and ops[n2]["q"] == "t":
                    after.add(n2)
                elif (w or w2) and clash(r, r2):
                    deps.add(n2)
                elif o[0] in PS and ops[n2]["q"] != q:
                    deps.add(n2)
        for w, o in both:
            r = (o[1], o[2], o[3])
            h = hist.setdefault(o[0], [])
            if w and o[0] not in PS:
                h[:] = [e for e in h if not (r[2] == 1 and r[0] <= e[0][0] and e[0][1] <= r[1] and e[2] != n)]
            h.append((r, w, n))
            if len(h) > 400:
                del h[:100]
        d = {"q": q, "call": call, "deps": deps, "after": after - deps, "cost": cost, "kind": kind, "ext": ext}
        if kind == "d":
            d["sem"] = "d%d" % ndma[0]
            ndma[0] += 1
        ops.append(d)
        return n

    CY = 0.00083 * 1.15

    def cols(o):
        return (o[2] - o[1] + o[3] - 1) // o[3]

    def vc(n, k=1.0):
        return 0.06 + max(64, n * k) * CY

    V, S, TE = g.vector, g.scalar, g.tensor

    def isap(x):
        return isinstance(x, tuple)

    def tt(out, a, c, o):
        k = 1.0 if (a[0] in PS or c[0] in PS) else 2.0
        op("v", lambda: V.tensor_tensor(out[4], a[4], c[4], o), [a, c], [out], vc(cols(out), k))

    def ts(out, a, s1, o1, s2=None, o2=None, ext=None):
        x1 = s1[4] if isap(s1) else s1
        x2 = s2[4] if isap(s2) else s2
        rd = [a] + [s for s in (s1, s2) if isap(s)]
        if o2 is None:
            op("v", lambda: V.tensor_scalar(out[4], a[4], x1, None, o1), rd, [out], vc(cols(out)), "c", ext)
        else:
            op("v", lambda: V.tensor_scalar(out[4], a[4], x1, x2, o1, o2), rd, [out], vc(cols(out)), "c", ext)

    def cp(out, a):
        op("v", lambda: V.tensor_copy(out[4], a[4]), [a], [out], vc(cols(out)))

    def scan(out, d0, d1, o0, o1):
        op("v", lambda: V.tensor_tensor_scan(out[4], d0[4], d1[4], 0.0, o0, o1), [d0, d1], [out], vc(cols(out)))

    def fill(out, x):
        op("v", lambda: V.memset(out[4], x), [], [out], vc(cols(out)))

    def act(out, a, f, bias=None, scale=1.0, extra=(), cost=None):
        kw = {"scale": scale}
        rd = [a] + list(extra)
        if bias is not None:
            kw["bias"] = bias[4] if isap(bias) else bias
            if isap(bias):
                rd.append(bias)
        op("s", lambda: S.activation(out[4], a[4], f, **kw), rd, [out], cost or (0.06 + cols(out) * CY))

    def mm(out, l, r, start=True, stop=True, f32=False):
        n = max(min(64, cols(l)), cols(r))
        op("t", lambda: TE.matmul(out[4], l[4], r[4], start, stop), [l, r], [out], 0.03 + n * (4 if f32 else 1) * 0.00083)

    def dma(q, out, src, reads, writes, us):
        eng = g.sync if q == "y" else g.scalar
        op(q, lambda: eng.dma_start(out, src), reads, writes, 0.06, "d", us)

    def iota(out, pat, base, cm, flag=False):
        kw = {"allow_small_or_imprecise_dtypes": True} if flag else {}
        op("g", lambda: g.iota(out[4], pat, base, cm, **kw), [], [out], 0.13 + 2 * cols(out) * CY)

    def load(q, name, lo, hi, src, rows=None):
        o = b(name, lo, hi, 1, rows)
        dma(q, o[4], src, [], [o], 2.5)

    load("y", "QF", 0, 768, T.q[:])
    load("s", "wi", 0, 1, T.w[:])
    load("y", "CHI", 0, 896, T.ch[:, 0:896])
    load("s", "CHI", 896, 1792, T.ch[:, 896:1792])
    load("y", "PT", 0, M, T.pt[:])
    load("s", "CHI", 1792, 2688, T.ch[:, 1792:2688])
    load("y", "r0i", 0, 768, T.r0[:], 8)
    load("s", "CHI", 2688, M, T.ch[:, 2688:M])
    load("y", "thi", 0, 1, T.th[:])

    iota(b("pi", 0, 1), [[0, 1]], 0, 1)
    iota(b("ji"), [[1, 128]], 0, 0)
    iota(b("c8"), [[1, 8]], 0, 0, True)
    ts(b("pi", 1, 2), b("pi", 0, 1), 15, OP.bitwise_and)
    ts(b("pi", 2, 3), b("pi", 0, 1), 4, OP.arith_shift_right)
    cp(b("pf", 0, 3), b("pi", 0, 3))
    P, P15, P4 = b("pf", 0, 1), b("pf", 1, 2), b("pf", 2, 3)
    cp(b("jf"), b("ji"))
    ts(b("j15i"), b("ji"), 15, OP.bitwise_and)
    cp(b("j15"), b("j15i"))
    ts(b("LC"), b("c8"), P4, OP.is_equal)
    ts(b("BLK"), b("LC"), 65536.0, OP.mult)
    cp(b("wf", 0, 1), b("wi", 0, 1))
    ts(b("WB"), b("LC"), b("wf", 0, 1), OP.mult)
    ts(b("D0", 0, 128), b("j15"), 0.0, OP.is_gt)
    ts(b("DM", 0, 128), b("j15"), P15, OP.is_equal)
    ts(b("IDF"), b("jf"), P, OP.is_equal)
    cp(b("IDB"), b("IDF"))
    ts(b("NIDB"), b("IDF"), -1.0, OP.mult)
    ts(b("RAMP"), b("j15"), 16.0 * 65536, OP.mult, 8.0 * 65536 - B24, OP.add)
    ts(b("MX"), b("D0", 0, 128), -2 * BIG, OP.mult, BIG, OP.add)
    ts(b("biasc", 0, 1), P15, 4096.0, OP.mult, -B24, OP.add)
    fill(b("C24"), B24)
    for h in "01":
        fill(b("SBD" + h), 0.0)
        fill(b("RBD" + h), 0.0)
    fill(b("V"), 32768)
    cp(b("r0f", rows=8), b("r0i", rows=8))
    for t in range(VI):
        for h in range(2):
            k = t * 2 + h
            mm(b("MC", 8 * k, 8 * k + 8), b("r0f", t * L + 128 * h, t * L + 128 * h + 128, rows=8), b("IDF", 0, 8, rows=8), f32=True)
    ts(b("R0P1"), b("MC", 0, 48), 1.0, OP.add)
    for k in range(4):
        cp(b("CH", 896 * k, 896 * k + 896), b("CHI", 896 * k, 896 * k + 896))
    fill(b("CH", M, ROOM), 0.0)
    fill(b("PT", 0, 1), 2048.0)
    cp(b("PT", M, M + L), b("QF", 0, L))
    fill(b("PT", M + L, 4096), 0.0)

    SBr = [b("VB", 0, 128), b("VB", 128, 256)]
    RBr = [b("VB", 256, 384), b("VB", 384, 512)]

    def lists(src, zt, mat, psum):
        tt(zt, src, mat, OP.mult)
        for x in range(cols(src) // 128):
            mm(b(psum, 8 * x, 8 * x + 8), b(zt[0], 128 * x, 128 * x + 128), b("LC"), f32=True)

    def radius(h):
        n = lambda x, *a: b(x + str(h), *a)
        ts(n("RBD", 0, 128, 16), n("Tf"), SC, OP.mult, (B24 + 524288) * SC, OP.add)
        scan(RBr[h], b("D0", 0, 128), n("RBD"), OP.mult, OP.add)

    def adopt(h, s, key):
        ti = b("V", 56 * h + s, 56 * h + 56, 7)
        tf = b("Tf%d" % h)
        tt(ti, key, tf, OP.min)
        ts(tf, ti, -65536, OP.bitwise_and)

    def begin(t, h, Q, Q16):
        hs = str(h)
        n = lambda x, *a: b(x + hs, *a)
        LI = "LI" + hs
        q = b(Q[0], Q[1] + 128 * h, Q[1] + 128 * h + 128)
        mm(b(LI, 8, 16), q, b("WB"))
        cp(n("si"), b(LI, 8, 16))
        ts(n("sj"), n("si"), 63, OP.bitwise_and)
        ts(n("SBD", 0, 128, 16), n("sj"), 1.0, OP.add)
        ts(n("RTL"), n("sj"), 32769.0, OP.add)
        scan(SBr[h], b("D0", 0, 128), n("SBD"), OP.mult, OP.add)
        lists(SBr[h], n("Z"), b("DM", 0, 128), LI)
        cp(n("OFF"), b(LI, 0, 8))
        for i in range(16):
            o = b(Q16, 2048 * h + i, 2048 * h + 2048, 16)
            if i < QSC:
                act(o, q, AF.Copy)
            else:
                cp(o, q)
        op("v", lambda: V.tensor_tensor(b("DR" + hs)[4], b("PT")[4].indirect(b("OFF" + hs)[4]), q[4], OP.subtract),
           [b("PT"), n("OFF"), q], [n("DR")], 0.05 + 128 * 1.5 * CY)
        act(n("DR"), n("DR"), AF.Abs)
        mm(b(LI, 16, 24), n("DR"), b("BLK"))
        tt(n("FB0"), b(LI, 16, 24), n("RTL"), OP.add)
        r1 = b("R0P1", 8 * (t * 2 + h), 8 * (t * 2 + h) + 8)
        if t == 0:
            ts(n("Tf"), r1, 65536.0, OP.mult, -B24 - 65536, OP.add)
        else:
            mm(b(LI, 24, 40), b("RF", 128 * h, 128 * h + 128), b("SELR"), f32=True)
            ts(n("ri"), b(LI, 24, 32), 0.0, OP.is_lt)
            tt(n("rx"), n("ri"), r1, OP.mult)
            tt(n("rho"), b(LI, 24, 32), n("rx"), OP.add)
            ts(b("BEST0", 8 * h, 8 * h + 8), b(LI, 32, 40), 0.0, OP.max)
            ts(n("Tf"), n("rho"), 65536.0, OP.mult, -B24, OP.add)
        radius(h)
        ts(n("SBD", 0, 128, 16), n("FB0"), -B24, OP.add)
        scan(SBr[h], b("D0", 0, 128), n("SBD"), OP.mult, OP.add)
        tt(n("E"), SBr[h], b("RAMP"), OP.subtract)
        act(n("A"), n("E"), AF.Abs, scale=SC)

    def push(t, h, s, Q16):
        hs = str(h)
        n = lambda x, *a: b(x + hs, *a)
        KP, LI = "KP" + hs, "LI" + hs
        kp = b(KP, 0, 128)
        ch = b("CH", 0, 4096)
        op("v", lambda: V.tensor_copy(n("PU")[4], ch[4].indirect(n("OFF")[4])), [ch, n("OFF")], [n("PU")], 0.05 + 128 * 1.5 * CY)
        act(n("Pf"), ind(ch, n("OFF")), AF.Identity, bias=b("biasc", 0, 1), extra=[n("OFF")], cost=0.065 + 128 * 1.5 * CY)
        tt(n("u"), n("A"), RBr[h], OP.subtract)
        if s == 0:
            adopt(h, 1, n("SBD", 0, 128, 16))
        mm(kp, n("Pf"), b("IDF"), True, False, f32=True)
        w = 2048 // NCH
        for c in range(NCH):
            lo = 2048 * h + w * c
            d = b("DIFF", lo, lo + w)
            o = n("PU", w // 16 * c, w // 16 * (c + 1))
            qq = b(Q16, lo, lo + w)
            if c in SCH[h]:
                act(d, ind(b("PT"), o), AF.Copy, extra=[o], cost=0.065 + w * 1.5 * CY)
                ps = ("MA", "MB", "MC")[rot[0] % 3]
                rot[0] += 1
                mm(b(ps, 0, w), b("IDB"), d, True, False)
                mm(b(ps, 0, w), b("NIDB"), qq, False, True)
                act(d, b(ps, 0, w), AF.Abs)
            else:
                op("v", lambda d=d, o=o, qq=qq: V.tensor_tensor(d[4], b("PT")[4].indirect(o[4]), qq[4], OP.subtract),
                   [b("PT"), o, qq], [d], 0.05 + w * 1.5 * CY)
                act(d, d, AF.Abs)
        for i in range(16):
            mm(b(KP, i, 128, 16), b("DIFF", 2048 * h + i, 2048 * h + 2048, 16), b("BLK"), False, i == 15)
        tt(n("KU"), kp, n("u"), OP.max)
        scan(n("KS"), b("MX"), n("KU"), OP.max, OP.min)
        adopt(h, s + 2, n("KS", 15, 128, 16))
        if s == 4:
            ts(b("RHO", 8 * h, 8 * h + 8), n("Tf"), 2.0 ** -16, OP.mult, 256.0, OP.add)
            return
        radius(h)
        tt(n("u2"), n("A"), RBr[h], OP.subtract)
        tt(n("KM"), kp, n("u2"), OP.max)
        scan(n("MS"), b("MX"), n("KM"), OP.max, OP.min)
        fb = (b("C24"), n("FB0"), n("FB1"), b("C24"))[s]
        tt(n("SBD", 0, 128, 16), n("MS", 15, 128, 16), fb, OP.min)
        scan(SBr[h], b("D0", 0, 128), n("SBD"), OP.mult, OP.add)
        lists(SBr[h], n("Z"), b("DM", 0, 128), LI)
        cp(n("lo"), b(LI, 0, 8))
        ts(n("lp"), n("lo"), 4095, OP.bitwise_and)
        cp(n("OFF"), n("lp"))
        if s in (0, 3):
            tt(n("E"), SBr[h], b("RAMP"), OP.subtract)
        else:
            ts(n("pm"), SBr[h], 0.0, OP.is_ge, -B24, OP.mult)
            tt(n("pm"), n("pm"), n("FO"), OP.mult)
            tt(n("pm"), n("pm"), b("RAMP"), OP.subtract)
            tt(n("E"), SBr[h], n("pm"), OP.add)
        act(n("A"), n("E"), AF.Abs, scale=SC)
        if s == 0:
            ts(n("FB1"), n("SBD", 0, 128, 16), B24, OP.add)
        if s in (0, 1):
            tt(n("OH"), n("KM"), SBr[h], OP.is_equal)
            act(n("FO"), n("OH"), AF.Identity, bias=1.0, scale=4096.0)

    def out_rows(src, buf, psum, out, t):
        for h in range(2):
            mm(b(psum, 128 * h, 128 * h + 128, 1, 8), b(src, 8 * h, 8 * h + 8), b("IDF"), f32=True)
        o = b(buf, 0, 256, 1, 8)
        act(o, b(psum, 0, 256, 1, 8), AF.Copy)
        dma("y", out[:, t * L:(t + 1) * L], o[4], [o], [], 2.0)

    def wide(vals, dst):
        vals(b("LBD2", 0, 256, 16))
        scan(b("VB", 0, 256), b("D0"), b("LBD2"), OP.mult, OP.add)
        lists(b("VB", 0, 256), b("Z3"), b("DM"), "MB")
        cp(b(dst), b("MB", 0, 16))

    def finish(t, Q):
        ts(b("VI"), b("V"), 65535, OP.bitwise_and)
        cp(b("VF"), b("VI"))
        ts(b("VZ"), b("VI"), 0.0, OP.is_equal)
        scan(b("LF"), b("VZ"), b("VF"), OP.mult, OP.add)
        last = b("LF", 6, 112, 7)
        if t < VI - 1:
            tt(b("FARB"), b("RHO"), b("TH"), OP.is_ge)
            mm(b("MA", 0, 8), b("LTRI"), b("FARB", 0, 8))
            mm(b("MA", 8, 16), b("LTRI"), b("FARB", 8, 16), True, False)
            mm(b("MA", 8, 16), b("ONESB"), b("FARB", 0, 8), False, True)
            ts(b("pl"), b("MA", 0, 16), float(CAP), OP.is_lt)
            tt(b("go"), b("pl"), b("FARB"), OP.mult)
            tt(b("gd"), b("MA", 0, 16), b("K192"), OP.subtract)
            tt(b("gd"), b("gd"), b("go"), OP.mult)
            tt(b("LBD", 0, 256, 16), b("gd"), b("K192"), OP.add)
            scan(b("VB", 256, 512), b("D0"), b("LBD"), OP.mult, OP.add)
            lists(b("VB", 256, 512), b("Z2"), b("DM"), "MB")
            cp(b("OFFP"), b("MB", 0, 16))
        cp(b("PI"), last)
        ts(b("PJ"), b("PI"), 4095, OP.bitwise_and)
        ts(b("ad"), last, 32768.0, OP.not_equal)
        ts(b("bn"), b("PJ"), 4096.0 * rank, OP.add)
        if t:
            tt(b("bn"), b("bn"), b("BEST0"), OP.subtract)
        tt(b("BEST"), b("bn"), b("ad"), OP.mult)
        if t:
            tt(b("BEST"), b("BEST"), b("BEST0"), OP.add)
        if t < VI - 1:
            ts(b("PK", 0, 256, 16), b("RHO"), 16.0, OP.mult)
            ts(b("PK", 1, 256, 16), b("BEST"), 16.0, OP.mult)
            for h in range(2):
                mm(b("MC", 128 * h, 128 * h + 128), b("PK", 128 * h, 128 * h + 128), b("IDF"), f32=True)
            tt(b("X"), b("MC", 0, 256), Q, OP.add)
            snd, rcv = "SND%d" % t, "RCV%d" % t
            op("v", lambda: V.tensor_copy(b(snd)[4].indirect(b("OFFP")[4]), b("X")[4]), [b("X"), b("OFFP")], [b(snd)], 0.05 + 256 * 3 * CY)
            dst = T.cores[(rank + 1) % N]
            rid, pid, _x = topo.addr(dst)
            op("g", lambda: g.remote_dma(T[rcv][:, 0:CAP], T[snd][:, 0:CAP], T.sem["arr%d" % t], T.sem["sent%d" % t], pid, rid, topo.mask(core, dst)),
               [b(snd, 0, CAP)], [], 0.1, "r", t)
        out_rows("RHO", "or%d" % t, "LI1", T.yr, t)
        out_rows("BEST", "ob%d" % t, "KP1", T.yb, t)
        if t == VI - 1:
            return
        cp(b("PN"), b("PJ"))
        ts(b("hi6"), b("PJ"), 4032, OP.bitwise_and)
        ts(b("lo6"), b("PJ"), 63, OP.bitwise_and)
        cp(b("NQ", 0, 16), b("hi6"))
        cp(b("NQ", 16, 32), b("lo6"))
        mm(b("KP1", 0, 128, 1, 32), b("NQ"), b("IDB"))
        act(b("NQT", 0, 128, 1, 32), b("KP1", 0, 128, 1, 32), AF.Copy)
        wide(lambda o: cp(o, b("PJ")), "GO1")
        act(b("GC"), ind(b("CH"), b("GO1")), AF.Copy, extra=[b("GO1")], cost=0.065 + 256 * 1.5 * CY)
        act(b("RHT"), b("MC", 0, 256), AF.Copy)
        for h in range(2):
            mm(b("LI0", 128 * h, 128 * h + 128), b("BC0"), b("RHT", 128 * h, 128 * h + 128))
        act(b("M1"), b("LI0", 0, 256), AF.Abs, bias=b("biasr", 0, 1))
        act(b("M1"), b("M1"), AF.Sign, scale=-1.0, bias=8.0)
        act(b("OHG"), b("M1"), AF.Relu)
        tt(b("OC"), b("OHG"), b("GC"), OP.mult)
        for h in range(2):
            mm(b("LI1", 8 * h, 8 * h + 8), b("OC", 128 * h, 128 * h + 128), b("LC"), f32=True)
        ts(b("emp"), b("LI1", 0, 16), 0.0, OP.is_equal)
        tt(b("can"), b("ad"), b("FARB"), OP.mult)
        tt(b("can"), b("can"), b("emp"), OP.mult)
        cp(b("CANB"), b("can"))
        for gg in range(8):
            ps, eq = ("MA", "KP0")[gg % 2], "EQ%d" % gg
            rw = [b("SELH", 128 * (8 * h + gg), 128 * (8 * h + gg) + 128, 1, 32) for h in range(2)]
            nt = b("NQT", 0, 128, 1, 32)
            mm(b(ps, 0, 128), rw[0], nt, True, False)
            mm(b(ps, 0, 128), b("IDB"), b("TRI"), False, True)
            mm(b(ps, 128, 256), rw[1], nt)
            mm(b(ps, 256, 384), rw[1], nt, True, False)
            mm(b(ps, 256, 384), b("IDB"), b("TRI"), False, True)
            for lo, hi, cc in ((0, 256, gg), (256, 384, 8 + gg)):
                if gg in GSC:
                    act(b("EF", lo, hi), b(ps, lo, hi), AF.Abs, scale=-1.0, bias=b("PN", cc, cc + 1))
                    act(b(eq, lo, hi), b("EF", lo, hi), AF.Relu, scale=-1.0, bias=1.0)
                else:
                    ts(b(eq, lo, hi), b(ps, lo, hi), b("PN", cc, cc + 1), OP.is_equal)
        for gg in range(8):
            eq = "EQ%d" % gg
            mm(b("MC", gg, gg + 1), b(eq, 0, 128), b("CANB", gg, gg + 1))
            mm(b("MC", 8 + gg, 9 + gg), b(eq, 128, 256), b("CANB", gg, gg + 1), True, False)
            mm(b("MC", 8 + gg, 9 + gg), b(eq, 256, 384), b("CANB", 8 + gg, 9 + gg), False, True)
        ts(b("win"), b("MC", 0, 16), 0.0, OP.is_equal)
        tt(b("win"), b("win"), b("can"), OP.mult)
        tt(b("YP"), b("win"), b("PN"), OP.mult)
        tt(b("gq"), b("PN"), b("K4096"), OP.subtract)
        tt(b("gq"), b("gq"), b("win"), OP.mult)
        wide(lambda o: tt(o, b("gq"), b("K4096"), OP.add), "GO2")
        tt(b("VAL"), b("OHG"), b("NID%d" % t), OP.mult)
        tt(b("VAL"), b("VAL"), b("GC"), OP.add)
        op("v", lambda: V.tensor_copy(b("CH")[4].indirect(b("GO2")[4]), b("VAL")[4]), [b("VAL"), b("GO2")], [b("CH")], 0.05 + 256 * 3 * CY)
        if t == 1:
            cp(b("PT", M + L, M + 2 * L), Q)
        out_rows("YP", "op%d" % t, "MB", T.yp, t)

    def receive(t):
        r = b("RCV%d" % (t - 1))
        ts(b("RV"), r, 0.0, OP.is_lt, ext=t - 1)
        ts(b("RI"), r, 15, OP.bitwise_and, ext=t - 1)
        tt(b("RT"), b("RV"), b("QF", L * t, L * t + L), OP.mult)
        tt(b("QV%d" % t), b("RT"), b("RI"), OP.add)
        ts(b("RS"), r, 4, OP.arith_shift_right, ext=t - 1)
        cp(b("RF"), b("RS"))

    def late_constants():
        cp(b("D0", 128, 256), b("D0", 0, 128))
        cp(b("DM", 128, 256), b("DM", 0, 128))
        ts(b("LTRI"), b("jf"), P, OP.is_gt)
        ts(b("TRI"), b("jf"), P, OP.is_le, 8192.0, OP.mult)
        fill(b("ONESB"), 1.0)
        fill(b("ONESF"), 1.0)
        ts(b("pf", 3, 4), P15, 0.0, OP.is_equal)
        ts(b("BLK0"), b("LC"), b("pf", 3, 4), OP.mult)
        ts(b("biasr", 1, 2), P15, 1.0, OP.is_equal)
        ts(b("SELR", 0, 8), b("LC"), b("pf", 3, 4), OP.mult)
        ts(b("SELR", 8, 16), b("LC"), b("biasr", 1, 2), OP.mult)
        ts(b("biasr", 0, 1), P15, -16.0, OP.mult, -7.5, OP.add)
        cp(b("thf", 0, 1), b("thi", 0, 1))
        ts(b("THM"), b("ONESF"), b("thf", 0, 1), OP.mult)
        mm(b("MC", 64, 72), b("THM"), b("BLK0"))
        cp(b("TH", 0, 8), b("MC", 64, 72))
        cp(b("TH", 8, 16), b("MC", 64, 72))
        iota(b("KI"), [[128, 2], [0, 8]], 0, 1, True)
        ts(b("K192"), b("KI"), float(CAP), OP.add)
        ts(b("K4096"), b("KI"), 4096.0, OP.add)
        iota(b("NID0"), [[1, 256]], M, 0, True)
        iota(b("NID1"), [[1, 256]], M + L, 0, True)
        iota(b("selj"), [[1, 16], [0, 128]], 0, 0, True)
        ts(b("SELH"), b("selj"), P15, OP.is_equal)
        ts(b("j15i"), b("ji"), 4, OP.arith_shift_right)
        cp(b("M1", 0, 128), b("j15i"))
        ts(b("M1", 0, 128), b("M1", 0, 128), P4, OP.is_equal, 0.0625, OP.mult)
        ts(b("BC0"), b("M1", 0, 128), b("pf", 3, 4), OP.mult)
        for x in ("LBD", "LBD2", "PK"):
            fill(b(x), 0.0)
        for x in "01":
            fill(b("SND" + x), -16)
            fill(b("RCV" + x, CAP, L), -16)

    for t in range(VI):
        Q = b("QF", 0, L) if t == 0 else b("QV%d" % t)
        Q16 = ("Q16a", "Q16b", "Q16a")[t]
        if t:
            receive(t)
        for h in range(2):
            begin(t, h, Q, Q16)
        if t == 0:
            late_constants()
        for s in range(5):
            for h in range(2):
                push(t, h, s, Q16)
        finish(t, Q)

    n = len(ops)
    WAKE = 0.06
    lat = [o["cost"] + (o["ext"] if o["kind"] == "d" else 0) for o in ops]
    succ = [[] for _ in range(n)]
    cnt = [0] * n
    for i, o in enumerate(ops):
        dd = set(o["deps"])
        if o["kind"] == "c" and o["ext"] is not None:
            x = [j for j in range(n) if ops[j]["kind"] == "r" and ops[j]["ext"] == o["ext"]][0]
            lat[x] = 4.0
            dd.add(x)
        for d in dd:
            succ[d].append((i, WAKE))
        for d in o["after"] - dd:
            succ[d].append((i, None))
        cnt[i] = len(dd | o["after"])
    pri = [0.0] * n
    for i in range(n - 1, -1, -1):
        pri[i] = max([lat[i] + x + pri[j] if x is not None else ops[i]["cost"] + pri[j] for j, x in succ[i]] or [lat[i]])
    rt = [0.0] * n
    free = {}
    order = []
    byq = {}
    for i in range(n):
        if cnt[i] == 0:
            byq.setdefault(ops[i]["q"], []).append(i)
    while len(order) < n:
        t0, qn = min((max(free.get(x, 0.0), min(rt[i] for i in lst)), x) for x, lst in byq.items() if lst)
        i = max((i for i in byq[qn] if rt[i] <= t0), key=lambda i: pri[i])
        byq[qn].remove(i)
        order.append(i)
        free[qn] = t0 + ops[i]["cost"]
        for j, x in succ[i]:
            if x is not None:
                rt[j] = max(rt[j], t0 + lat[i] + x)
            cnt[j] -= 1
            if cnt[j] == 0:
                byq.setdefault(ops[j]["q"], []).append(j)

    QS = {"v": V, "t": TE, "s": S, "g": g, "y": g.sync}
    CS = {"v": "cv", "t": "ct", "s": "cs", "g": "cg"}
    done = {}
    total = {"v": 0, "t": 0, "s": 0, "g": 0}
    know = {x: {} for x in QS}
    nout = len(topo.engines(core, T.cores[(rank + 1) % N]))
    nin = len(topo.engines(T.cores[(rank - 1) % N], core))
    for i in order:
        o = ops[i]
        qn = o["q"]
        k = know[qn]
        need = {}
        for d in o["deps"]:
            sem, val, kn = done[d]
            if need.get(sem, (0,))[0] < val:
                need[sem] = (val, kn)
        if o["kind"] == "c" and o["ext"] is not None:
            need["arr%d" % o["ext"]] = (nin, {})
        for sem, (val, kn) in sorted(need.items(), key=lambda e: -len(e[1][1])):
            if k.get(sem, 0) >= val:
                continue
            QS[qn].wait_ge(T.sem[sem], val)
            k[sem] = val
            for a, c in kn.items():
                if k.get(a, 0) < c:
                    k[a] = c
        if o["kind"] == "c":
            total[qn] += 1
            o["call"]().then_inc(T.sem[CS[qn]], 1)
            done[i] = (CS[qn], total[qn], dict(k))
        elif o["kind"] == "d":
            o["call"]().then_inc(T.sem[o["sem"]], 16)
            done[i] = (o["sem"], 16, dict(k))
        else:
            o["call"]()
            done[i] = ("sent%d" % o["ext"], nout, dict(k))
    for x in "vtsg":
        g.wait_ge(T.sem[CS[x]], total[x])
    for i in range(ndma[0]):
        g.wait_ge(T.sem["d%d" % i], 16)
    for t in range(VI - 1):
        g.wait_ge(T.sem["sent%d" % t], nout)
        g.wait_ge(T.sem["arr%d" % t], nin)
    return max(free.values())
